import numpy as np, ml_dtypes
CORES = [16,18,20,22]
N = 4
BF = ml_dtypes.bfloat16
V, T, BACK, HOPS = 3584, 256, 0, (1, 1, 1, 1, 1, 1)
def wanted(rng, pm, n, share, e):
    u = rng.random((N, 8, 16, n)); v = np.where(rng.random((N, 8, 16, n)) < share, V * u ** e, V * u).astype(np.int64)
    return pm[np.arange(8)[:, None, None], np.minimum(v, V - 1)]
def parts(rng, share=0.3, e=4.0):
    pm = np.argsort(rng.random((8, V)), axis=-1)
    return (rng.integers(0, 16, (N, 8, 16, V)), rng.integers(0, 16, (N, 8, 16, V)), wanted(rng, pm, V, share, e),
            rng.integers(0, 16, (N, 8, 16, T)), wanted(rng, pm, T, share, e), rng.integers(10, 45, (N, 8, 1)), pm)
def worst(x):
    return np.where(x < 8, 15, 0)
def apart(x, d):
    c = x.copy(); left = d.copy()
    for i in range(16):
        up = 15 - x[i] >= x[i]; m = np.minimum(left, np.where(up, 15 - x[i], x[i]))
        c[i] = np.where(up, x[i] + m, x[i] - m); left = left - m
    return c
def pack(x, y, ap, c, al, th):
    def b(a): return np.ascontiguousarray(a.reshape(N, 128, -1)).astype(np.float32).astype(BF)
    def w(a): return np.ascontiguousarray(a.reshape(N, 128, -1)).astype(np.int32)
    return {"fx": b(x), "hx": b(y), "ha": w(ap), "vx": b(c), "va": w(al), "th": th.astype(np.int32)}
def setup_inputs(rng):
    x, y, ap, c, al, th, pm = parts(rng)
    return pack(x, y, ap, c, al, th)
def setup_inputs_ties(rng):
    x, y, ap, c, al, th, pm = parts(rng, 0.5, 6.0); s = rng.integers(1, 4, (1, 8, 1, 1))
    x = (x & 1) * s; y = (y & 1) * s; c = (c & 1) * s; th = s[:, :, 0] * rng.integers(0, 5, (N, 8, 1))
    i = rng.integers(0, T // 2, T); c[:, ::2] = c[:, ::2][..., i]; al[:, ::2] = al[:, ::2][..., i]
    ap[:, :, 8:] = ap[:, :, :8]; al[:, 1::2, 8:] = al[:, 1::2, :8]
    return pack(x, y, ap, c, al, th)
def setup_inputs_crowd(rng):
    x, y, ap, c, al, th, pm = parts(rng)
    n = rng.permutation(np.array([1, 2, 3, 7, 16, 64, 256, V // 2]))
    for g in range(8):
        q = pm[g, :n[g]]
        y[:, g][:, :, q] = worst(x[:, g][:, :, q])
        ap[:, g] = q[rng.integers(0, n[g], (N, 16, V))]; al[:, g] = q[rng.integers(0, n[g], (N, 16, T))]
    i = rng.integers(0, T // 4, T); j = int(np.argmin(n)); c[:, ::2] = c[:, ::2][..., i]; c[:, j] = c[:, j][..., rng.permutation(i)]
    return pack(x, y, ap, c, al, rng.integers(0, 12, (N, 8, 1)))
def setup_inputs_ends(rng):
    x, y, ap, c, al, th, pm = parts(rng); o = rng.permutation(8); h = V // 2
    g = o[0]
    ap[:, g] = rng.integers(0, 2, (N, 16, V)) * (V - 1); al[:, g] = rng.integers(0, 2, (N, 16, T)) * (V - 1)
    y[:, g][:, :, [0, V - 1]] = worst(x[:, g][:, :, [0, V - 1]]); th[:, g] = rng.integers(0, 6, (N, 1))
    g = o[1]
    p = rng.integers(0, 2, (16, 1)) * 15; x[:, g] = p; y[:, g] = 15 - p; c[:, g] = p; th[:, g] = 240
    g = o[2]
    for q in range(N):
        f = rng.permutation(V)[:T]; d = rng.integers(60, 101, T); more = rng.permutation(np.arange(T) & 1)
        y[q, g][:, f] = apart(x[q, g][:, f], d); c[q, g] = apart(x[q, g][:, f], d - th[q, g, 0] - more); al[q, g] = f[None, :]
    g = o[3]
    p = rng.integers(0, 2, (16, 1)) * 15; x[:, g] = p; y[:, g] = 15 - p; c[:, g] = p; th[:, g] = 239
    g = o[4]
    x[:, g] = np.where(rng.random((N, 16, V)) < 0.5, 0, x[:, g]); y[:, g] = x[:, g]; y[:, g][:, :, :h] = worst(x[:, g][:, :, :h]); th[:, g] = rng.integers(0, 20, (N, 1))
    for a, n in ((ap, V), (al, T)):
        a[:, g] = rng.integers(h, V, (N, 16, n)); m = rng.random((N, n)) < 0.5; v = rng.integers(0, h, (N, n))
        a[:, g, 0] = np.where(m, v, a[:, g, 0]); a[:, g, 15] = np.where(m, a[:, g, 15], v)
    g = o[5]
    ap[:, g] = ap[:, g, :1]; al[:, g] = al[:, g, :1]
    g = o[6]
    y[:, g] = x[:, g]; th[:, g] = 0
    for q in range(N):
        f = rng.integers(0, V, T); m = rng.random(T) < 0.75
        al[q, g] = f[None, :]; c[q, g] = np.where(m[None, :], x[q, g][:, f], c[q, g])
    g = o[7]
    y[:, g] = x[:, g]; th[:, g] = rng.integers(0, 16, (N, 1)); R = len(HOPS); S = [sum(HOPS[:j]) for j in range(R)]
    o7 = rng.permutation(V); rest = o7[N + N * R:]
    ap[:, g] = rest[rng.integers(0, len(rest), (N, 16, V))]; al[:, g] = rest[rng.integers(0, len(rest), (N, 16, T))]
    for q in range(N):
        a = o7[q]; y[q, g][:, [a]] = apart(x[q, g][:, [a]], np.array([120]))
        for j in range(R):
            s = (q - S[j]) % N; t = q * R + j; home = apart(x[q, g][:, [a]], np.array([104 - 16 * j]))[:, 0]
            way = [(s + S[i]) % N for i in range(j)]; seen = [i for i in range(j) if way[i] == q]
            if not seen:
                c[s, g, :, t] = home; al[s, g, :, t] = a
            else:
                w = [way[m] for m in range(seen[-1] + 1, j) if way[m] not in way[:m]][0]; b = o7[N + t]
                x[w, g, :, b] = worst(home); y[w, g, :, b] = home; ap[w, g, :, b] = a
                c[s, g, :, t] = x[w, g, :, b]; al[s, g, :, t] = b
    return pack(x, y, ap, c, al, th)
def setup_inputs_full(rng):
    x, y, ap, c, al, th, pm = parts(rng); y = x.copy(); th = rng.integers(0, 60, (N, 8, 1)); z = rng.integers(0, 2, 8); q0 = int(rng.integers(0, N))
    for q in range(N):
        kinds = rng.permutation(np.array([0, 0, 1, 2, 3, 3, 4, 4]))
        for g in range(8):
            e = int(z[g] + q) % 2; kind = 0 if q == q0 else int(kinds[g])
            y[q, g][:, e::2] = worst(x[q, g][:, e::2]); far = e + 2 * rng.permutation(V // 2)
            f = far[:T]; d = rng.integers(0, 60, T)
            if kind == 1:
                n = min(T, V // 16); r = e + 2 * int(rng.integers(0, 8)); f = rng.permutation((r + 16 * rng.permutation(V // 16)[:n])[np.arange(T) % n])
            if kind == 2:
                f = e + 2 * (rng.permutation(T) + int(rng.integers(0, 2)) * (V // 2 - T))
            if kind == 3:
                tt = np.sort(rng.permutation(T).reshape(-1, 2), axis=1); f = np.zeros(T, np.int64); f[tt] = far[:T // 2][:, None]; d[tt] = rng.integers(0, 30, tt.shape) + np.array([30, 0])
            if kind == 4:
                a = far[0]; x[q, g, :, a] = 15 * rng.integers(0, 2, 16); y[q, g, :, a] = 15 - x[q, g, :, a]; th[q, g] = 0
                f = np.full(T, a); d = np.maximum(min(T, 240) - 1 - np.arange(T), 0)
            c[q, g] = apart(x[q, g][:, f], d); al[q, g] = f[None, :]
    return pack(x, y, ap, travel(c, -HOPS[0]), travel(al, -HOPS[0]), th)
def setup_inputs_spread(rng):
    x, y, ap, c, al, th, pm = parts(rng)
    def f(n): return np.minimum((np.exp2(4 * rng.random((N, 8, 1, n))) * rng.random((N, 8, 16, n)) + 0.5).astype(np.int64), 15)
    x = f(V); y = f(V); c = f(T); y = np.where(rng.random((N, 8, 1, V)) < 0.1, worst(x), y)
    ap = wanted(rng, pm, V, 0.8, np.exp2(4 * rng.random((N, 8, 1, V)))); al = wanted(rng, pm, T, 0.8, np.exp2(4 * rng.random((N, 8, 1, T))))
    th = (120 * rng.random((N, 8, 1)) ** 3).astype(np.int64); th[:, rng.integers(0, 8)] = 0
    return pack(x, y, ap, c, al, th)
def check_inputs(d):
    bad = []
    for k in ("fx", "hx", "vx"):
        v = np.asarray(d[k]).astype(np.float64)
        if not np.all((v >= 0) & (v <= 15) & (v == np.floor(v))): bad.append("whole numbers of " + k)
    for k, hi in (("ha", V - 1), ("va", V - 1), ("th", 240)):
        if np.min(d[k]) < 0 or np.max(d[k]) > hi: bad.append("range of " + k)
    return bad
def travel(a, h):
    b = np.roll(a, h, axis=0)
    if BACK: b[..., T - BACK:] = np.roll(a[..., T - BACK:], -h, axis=0)
    return b
def reference(fx, hx, ha, vx, va, th):
    x = fx.astype(np.float32).astype(np.int32).reshape(N, 8, 16, V)
    y = hx.astype(np.float32).astype(np.int32).reshape(N, 8, 16, V)
    ap = ha.astype(np.int64).reshape(N, 8, 16, V)
    hid = np.zeros((N, 8, V), np.int64) + np.arange(N)[:, None, None] * V + np.arange(V)
    c = vx.astype(np.float32).astype(np.int32).reshape(N, 8, 16, T)
    al = va.astype(np.int64).reshape(N, 8, 16, T)
    tid = np.zeros((N, 8, T), np.int64) + N * V + np.arange(N)[:, None, None] * T + np.arange(T)
    length = np.zeros((N, 8, T), np.int64); lim = th.astype(np.int64)
    ri = np.arange(N)[:, None, None]; gi = np.arange(8)[None, :, None]
    for h in HOPS:
        own = np.add.reduce(np.abs(x - y), axis=2)
        xa = np.take_along_axis(x, al.reshape(N, 8, 1, 16 * T), 3).reshape(N, 8, 16, 16, T)
        there = np.add.reduce(np.abs(xa - c[:, :, :, None, :]), axis=2)
        gain = np.take_along_axis(own, al.reshape(N, 8, 16 * T), 2).reshape(N, 8, 16, T).astype(np.int64) - there
        k = np.argmax(gain, axis=2)[:, :, None]
        best = np.take_along_axis(gain, k, 2)[:, :, 0]; fam = np.take_along_axis(al, k, 2)[:, :, 0]
        offer = best > lim
        key = np.where(offer, best * T + (T - 1 - np.arange(T)), -1)
        top = np.full((N, 8, V), -1, np.int64); np.maximum.at(top, (ri, gi, fam), key)
        n_, g_, t_ = np.nonzero(offer & (np.take_along_axis(top, fam, 2) == key)); f_ = fam[n_, g_, t_]
        old = y[n_, g_, :, f_]; y[n_, g_, :, f_] = c[n_, g_, :, t_]; c[n_, g_, :, t_] = old
        old = ap[n_, g_, :, f_]; ap[n_, g_, :, f_] = al[n_, g_, :, t_]; al[n_, g_, :, t_] = old
        old = hid[n_, g_, f_]; hid[n_, g_, f_] = tid[n_, g_, t_]; tid[n_, g_, t_] = old
        length[n_, g_, t_] += 1
        c = travel(c, h); al = travel(al, h); tid = travel(tid, h); length = travel(length, h)
    return {"yh": hid.astype(np.float32), "yt": tid.astype(np.float32), "yl": length.astype(np.float32)}

from concourse.bass import DstId, RemoteDMATransfer
from concourse.mybir import AluOpType as A, AxisListType, ActivationFunctionType as F

V, TK, R = 3584, 256, 6
W = V + TK
C0 = 12 * 65536
F32, BF, I32, U16 = "float32", "bfloat16", "int32", "uint16"
CHUNKS = (2, 2, 2, 2, 2, 2, 1, 1)

SCRATCH = {}
for _d, _l in (
        (BF, "X2:7168 Y:3840 MN:3584 GA:4096 GB:4096 GX:1024 U:256 WC:512 WB:16 WA:128 WY:256 SEL:512 IB:128 NI:128 "
             "KL:256 RT:16 ON:128 RR:256 LE:256 LO:256 scc:768"),
        (F32, "S:3840 J:272 J15:256 J4:256 JS:32 PC:8 PD:32 RW:112 U0:272 HM:272 WD:16 WK:256 IF:128 EA:128 MK:256 "
              "D0:256 PK:8 KM:256 KS:256 THF:8 LS:64 SC:256 L:160 O1:16 RK:256 G32:256 NN:256 APF:256 TT:256 AD:256 "
              "smeta:32 OUT:128"),
        (I32, "AP:3840 PI:8 T2:272 T3:272 THS:8 KI:16 FI:16 GI:16"),
        (U16, "OFS:32 O:32 FO:16 soff:256 saln:256")):
    for _x in _l.split():
        SCRATCH[_x.split(":")[0]] = ("sbuf", [128, int(_x.split(":")[1])], _d)
for _r in range(R):
    SCRATCH["off%d" % _r] = ("sbuf", [128, 256], U16)
    SCRATCH["aln%d" % _r] = ("sbuf", [128, 256], U16)
    SCRATCH["cc%d" % _r] = ("sbuf", [128, 768], BF)
for _r in range(R + 1):
    SCRATCH["meta%d" % _r] = ("sbuf", [128, 32], F32)
for _r in range(8):
    SCRATCH["B%d" % _r] = ("psum", [128, 512], F32)

SEMAPHORES = ["ev", "es", "et", "eg", "lx0", "lx1", "lx2", "ly0", "ly1", "lap", "lva", "lvx", "lvc", "lth", "o1", "o2"]
for _r in range(R):
    SEMAPHORES += [_x % _r for _x in ("a%d", "b%d", "c%d", "m%d", "sa%d", "sb%d", "sc%d", "sm%d", "yc%d")]


def rank_program(g, core, T, topo):
    rank = T.rank_of(core)
    if rank is None:
        return
    n = len(T.cores)
    nxt = T.cores[(rank + 1) % n]
    rid, pid = topo.addr(nxt)[:2]
    eng = topo.engines(core, nxt)

    Q = {"v": g.vector, "s": g.scalar, "t": g.tensor, "g": g, "y": g.sync}
    count = {}
    known = {e: {} for e in Q}
    lastw, readers, clock = {}, {}, {}

    def need(e, tok):
        sem, val = tok
        if known[e].get(sem, 0) >= val:
            return
        Q[e].wait_ge(T.sem[sem], val)
        known[e][sem] = val
        for s2, v2 in clock.get(tok, {}).items():
            if known[e].get(s2, 0) < v2:
                known[e][s2] = v2

    def before(e, rd, wr):
        toks = []
        for k in rd:
            if k in lastw:
                toks.append(lastw[k])
            if k[0] == "B" and k[1:].isdigit():
                toks += [x for x in readers.get(k, []) if x[0] != "e" + e]
        for k in wr:
            if k in lastw:
                toks.append(lastw[k])
            toks += readers.get(k, [])
        for tok in sorted(toks, key=lambda x: -x[1]):
            if not (e == "t" and tok[0] == "et"):
                need(e, tok)

    def after(e, tok, rd, wr):
        clock[tok] = dict(known[e])
        for k in rd:
            readers.setdefault(k, []).append(tok)
        for k in wr:
            lastw[k] = tok
            readers[k] = []

    def op(e, rd, wr, fn, *a, **kw):
        rd, wr = rd.split(), wr.split()
        before(e, rd, wr)
        sem = "e" + e
        count[sem] = count.get(sem, 0) + 1
        fn(*a, **kw).then_inc(T.sem[sem], 1)
        after(e, (sem, count[sem]), rd, wr)

    def dma(e, sem, rd, wr, pairs, **kw):
        rd, wr = rd.split(), wr.split()
        before(e, rd, wr)
        for o, i in pairs:
            Q[e].dma_start(o, i, **kw).then_inc(T.sem[sem], 16)
            count[sem] = count.get(sem, 0) + 16
        after(e, (sem, count[sem]), rd, wr)

    def send(sem, rd, lands, src, dst):
        rd = rd.split()
        before("g", rd, [])
        g.remote_dma(dst, src, T.sem[sem], T.sem["s" + sem], pid, rid, topo.mask(core, nxt))
        count[sem] = count["s" + sem] = len(eng)
        after("g", ("s" + sem, len(eng)), rd, [])
        for k in lands.split():
            lastw[k] = (sem, len(eng))

    def ts(rd, wr, out, in0, s1, s2, o0, o1=None):
        if o1 is None:
            op("v", rd, wr, g.vector.tensor_scalar, out, in0, s1, None, o0)
        else:
            op("v", rd, wr, g.vector.tensor_scalar, out, in0, s1, s2, o0, o1)

    def tt(rd, wr, out, a, b, o):
        op("v", rd, wr, g.vector.tensor_tensor, out, a, b, o)

    def cp(rd, wr, out, a):
        op("v", rd, wr, g.vector.tensor_copy, out, a)

    def ms(wr, out, c):
        op("v", "", wr, g.vector.memset, out, c)

    def mm(rd, wr, out, l, r, st, sp):
        op("t", rd, wr, g.tensor.matmul, out, l, r, st, sp)

    def act(rd, wr, out, a, f=F.Identity, **kw):
        op("s", rd, wr, g.scalar.activation, out, a, f, **kw)

    def iota(wr, out, pat, base, cm):
        op("g", "", wr, g.iota, out, pat, base, cm, allow_small_or_imprecise_dtypes=True)

    B = [T["B%d" % i] for i in range(8)]
    eq, mul, add, sub = A.is_equal, A.mult, A.add, A.subtract

    dma("y", "lva", "", "APt", [(T.AP[:, V:W], T.va[:])])
    dma("s", "lvc", "", "cn0", [(T.cc0[:, 0:256], T.vx[:])])
    for j, (lo, hi) in enumerate(((0, 1536), (1536, V))):
        dma("y", "lx%d" % j, "", "X1%d" % j, [(T.X2[:, lo:hi], T.fx[:, lo:hi])])
        dma("s", "ly%d" % j, "", "Y%d" % j, [(T.Y[:, lo:hi], T.hx[:, lo:hi])])
    dma("y", "lx2", "X10 Y0", "X2", [(T.X2[16 * q:16 * q + 16, V:2 * V], T.fx[16 * (q ^ 1):16 * (q ^ 1) + 16, :]) for q in range(8)])
    dma("y", "lvx", "", "Yt", [(T.Y[:, V:W], T.vx[:])])
    dma("y", "lap", "X2 X11 Y1", "AP", [(T.AP[:, 0:V], T.ha[:])])

    op("g", "", "PI0", g.iota, T.PI[:, 0:1], [[0, 1]], 0, 1)
    iota("J", T.J[:, 0:256], [[1, 256]], 0, 0)
    iota("J2", T.J[:, 256:272], [[256, 16]], 0, 0)
    iota("JS0", T.JS[:, 0:16], [[16, 8], [128, 2]], 0, 0)
    iota("AD", T.AD[:], [[0, 8], [1, 2], [0, 16]], 0, 0)
    iota("J15", T.J15[:], [[0, 16], [1, 16]], 0, 0)
    iota("St", T.S[:, V:W], [[0, 256]], 0, 0)
    iota("J4", T.J4[:], [[1, 16], [0, 16]], 0, 0)
    iota("BL", T.LS[:, 0:16], [[128, 2], [0, 8]], V, 1)
    iota("NK", T.LS[:, 16:32], [[128, 2], [0, 8]], -(C0 + 255), 1)
    iota("NV", T.LS[:, 32:48], [[0, 4], [-1, 2], [0, 2]], 0, 0)
    iota("J7", T.JS[:, 16:32], [[0, 2], [1, 8]], 0, 0)
    iota("meta0", T.meta0[:, 0:16], [[128, 2], [0, 8]], n * V + rank * TK, 1)
    iota("meta0", T.meta0[:, 16:32], [[0, 16]], 0, 0)
    iota("KL", T.KL[:], [[0, 256]], 0, 0)
    iota("KM", T.KM[:], [[0, 256]], 0, 0)
    iota("ON", T.ON[0:8, :], [[0, 128]], 1, 0)
    dma("g", "lth", "", "THS", [(T.THS[0:8, 0:1], T.th[:])], allow_slow_non_contiguous=True)

    rw = lambda j: T.RW[:, 16 * j:16 * j + 16]
    for j, c in ((0, 0.5), (1, 2.0), (2, 0.0), (5, -256.0)):
        ms("RW%d" % j, rw(j), c)
    op("v", "RW0 RW2", "RW3", g.vector.tensor_tensor_scan, rw(3), rw(0), rw(2), 2.0, mul, add)
    op("v", "RW1 RW2", "RW4", g.vector.tensor_tensor_scan, rw(4), rw(1), rw(2), 2.0 ** -10, mul, add)
    pi = lambda j: T.PI[:, j:j + 1]
    ts("PI0", "PI1", pi(1), pi(0), 15, None, A.bitwise_and)
    ts("PI0", "PI2", pi(2), pi(0), 4, None, A.arith_shift_right)
    ts("PI0", "PI3", pi(3), pi(0), 4, 1, A.arith_shift_right, A.bitwise_and)
    ts("PI0", "PI4", pi(4), pi(0), 5, None, A.arith_shift_right)
    ts("PI0", "PI5", pi(5), pi(0), 7, None, A.bitwise_and)
    ts("PI0", "PI6", pi(6), pi(0), 3, 1, A.arith_shift_right, A.bitwise_and)
    for j, (a, b) in enumerate(((248.0, 256.0), (-0.5, 1.0), (65536.0, 0.0), (0.0, float(rank * V)))):
        op("v", "RW4 RW5", "RW4_%d" % j, g.vector.memset, T.RW[:, 76 + j:77 + j], a)
        op("v", "RW4 RW5", "RW5_%d" % j, g.vector.memset, T.RW[:, 92 + j:93 + j], b)
    cp("PI0 PI1 PI2 PI3 PI4 PI5 PI6", "PC", T.PC[:, 0:7], T.PI[:, 0:7])
    p, r_, gi_, par, qd = [T.PC[:, j:j + 1] for j in range(5)]
    names = {}

    def pd(name, in0, s1, s2, o0, o1=None, rd=""):
        names[name] = T.PD[:, len(names):len(names) + 1]
        ts("PC " + rd, name, names[name], in0, s1, s2, o0, o1)
        return names[name]

    J16, J128 = T.J[:, 0:16], T.J[:, 0:128]
    amp = pd("amp", r_, 12.0, 512.0, A.is_lt, mul)
    m15 = pd("m15", r_, 15.0, None, eq)
    d14 = pd("d14", gi_, 16.0, 14.0, mul, add)
    w1 = pd("w1", r_, 12.0, -16.0, eq, mul)
    nr = pd("nr", r_, -1.0, None, mul)
    nv = pd("nv", par, -float(V), None, mul)
    ts("J PC", "RW6", rw(6), J16, r_, None, eq)
    act("J J2 m15", "HM", T.HM[:], T.J[:], scale=m15)
    for j in (3, 4, 5):
        tt("RW6 RW%d " % j + " ".join("RW%d_%d" % (j, i) for i in range(4)), "RW%d" % j, rw(j), rw(j), rw(6), mul)
    for j, nm in ((3, "sr"), (4, "w0"), (5, "cw")):
        names[nm] = T.PD[:, len(names):len(names) + 1]
        op("v", "RW%d" % j, nm, g.vector.tensor_reduce, names[nm], rw(j), AxisListType.X, add)
    ts("J J2 sr", "T2", T.T2[:], T.J[:], names["sr"], -(0.5 - 2.0 ** -13), mul, add)
    ts("J PC", "IB", T.IB[:], J128, p, None, eq)
    ts("T2", "T3", T.T3[:], T.T2[:], 1, None, A.bitwise_and)
    ts("J d14", "WY0", T.WY[:, 0:128], J128, d14, None, eq)
    ts("T3 amp", "U0", T.U0[:], T.T3[:], amp, None, mul)
    ts("J d14", "WY1", T.WY[:, 128:256], J128, d14, -2.0, eq, mul)
    tt("U0 HM", "U1", T.U0[:, 256:272], T.U0[:, 256:272], T.HM[:, 256:272], add)
    tt("U0 HM", "U", T.U[:], T.U0[:, 0:256], T.HM[:, 0:256], add)
    ts("U1 cw", "WD", T.WD[:], T.U0[:, 256:272], names["cw"], None, add)
    x16 = pd("x16", T.PC[:, 6:7], 16.0, None, mul)
    even = pd("even", par, -1.0, 1.0, mul, add)
    pp = pd("pp", p, 16.0, None, add)
    pm = pd("pm", p, -16.0, None, add)
    dperm = pd("dperm", T.PC[:, 5:6], 32.0, x16, mul, add, "x16")
    act("IB", "IF", T.IF[:], T.IB[:])
    act("IB", "NI", T.NI[:], T.IB[:], scale=-1.0)
    act("AD nv", "AD", T.AD[:], T.AD[:], F.Abs, scale=float(V), bias=nv)
    act("J15 nr", "MK", T.MK[:], T.J15[:], F.Abs, bias=nr)
    act("J15", "D0", T.D0[:], T.J15[:], F.Sign)
    act("J15 w1 w0", "WK", T.WK[:, 0:128], T.J15[:, 0:128], scale=w1, bias=names["w0"])
    act("MK", "MK", T.MK[:], T.MK[:], F.Relu, scale=-1.0, bias=1.0)
    cp("APt", "aln0", T.aln0[:], T.AP[:, V:W])
    for j, (tg, mk) in enumerate(((p, even), (pp, even), (pm, par), (p, par))):
        ts("J PC even pp pm", "SEL%d" % j, T.SEL[:, 128 * j:128 * j + 128], J128, tg, mk, eq, mul)

    def turn(win, kwin, off, koff):
        tt(kwin + " O AD", "APF", T.APF[:], win.indirect(T.O[:, 16:32]), T.AD[:], add)
        op("v", "APF", "TT", g.vector.transpose, T.TT[:], T.APF[:])
        cp("TT PERMO", koff, off, T.TT[:].indirect(T.OFS[:, 16:32]))

    def features_out(cc, kcn, kca):
        for c in range(2):
            for h in range(2):
                j = 2 * c + h
                mm(kcn + " SEL%d" % j, "B4", B[4][:, 128 * c:128 * c + 128], T.SEL[:, 128 * j:128 * j + 128],
                   cc[:, 128 * h:128 * h + 128], h == 0, h == 1)
        for j in range(1, 3):
            act("B4", kca + "_%d" % j, cc[:, 256 * j:256 * j + 256], B[4][:, 0:256])

    features_out(T.cc0, "cn0", "ca0")
    for j in range(7):
        lo, bk, hf = 512 * j, 5 + j % 3, int(j >= 3)
        tt("X1%d Y%d" % (hf, hf), "MN%d" % j, T.MN[:, lo:lo + 512], T.X2[:, lo:lo + 512], T.Y[:, lo:lo + 512], A.min)
        mm("Y%d WY0" % hf, "B%d" % bk, B[bk][:], T.WY[:, 0:128], T.Y[:, lo:lo + 512], True, False)
        for u in range(2):
            mm("U IB", "B%d" % bk, B[bk][:, 256 * u:256 * u + 256], T.IB[:], T.U[:], False, False)
        mm("MN%d WY1" % j, "B%d" % bk, B[bk][:], T.WY[:, 128:256], T.MN[:, lo:lo + 512], False, True)
        for u in range(2):
            act("B%d WD" % bk, "S%d" % (2 * j + u), T.S[:, lo + 256 * u:lo + 256 * u + 256],
                B[bk][:, 256 * u:256 * u + 256], bias=T.WD[:, 2 * j + u:2 * j + u + 1])
    SK = " ".join("S%d" % j for j in range(14)) + " St"
    ts("JS0 PC", "O", T.O[:, 16:32], T.JS[:, 0:16], r_, None, add)
    ts("J dperm", "PERMO", T.OFS[:, 16:32], J16, dperm, None, add)
    a8 = pd("a8", par, 8.0, None, mul)
    turn(T.AP[:, V:W], "APt", T.off0[:], "off0")

    a4 = pd("a4", par, 4.0, qd, mul, add)
    n13 = pd("n13", r_, 13.0, -1.0, eq, mul)
    tb0 = pd("tb0", qd, 2.0, a8, mul, add, "a8")
    odd = pd("odd", r_, 14.0, par, A.is_lt, mul)
    g8 = pd("g8", gi_, 8.0, None, add)
    tb1 = pd("tb1", tb0, 1.0, None, add, None, "tb0")
    g2 = pd("g2", gi_, 2.0, None, mul)
    g21 = pd("g21", gi_, 2.0, 1.0, mul, add)
    kb = pd("kb", w1, 16.0, n13, mul, add, "w1 n13")
    ts("J4 PC", "WK1", T.WK[:, 128:256], T.J4[:, 0:128], gi_, None, eq)
    ts("J4 tb0", "WC0", T.WC[:, 0:256], T.J4[:], tb0, -65536.0, eq, mul)
    ts("J4 tb1", "WC1", T.WC[:, 256:512], T.J4[:], tb1, -65536.0, eq, mul)
    ts("J a4", "WB0", T.WB[:, 0:8], T.J[:, 0:8], a4, 131072.0, eq, mul)
    ts("J a4", "WB1", T.WB[:, 8:16], T.J[:, 0:8], a4, -131072.0, eq, mul)
    tt("WK WK1", "WA", T.WA[:], T.WK[:, 0:128], T.WK[:, 128:256], mul)
    cp("THS", "THF", T.THF[0:8, 0:1], T.THS[0:8, 0:1])
    cp("J", "REPO", T.OFS[:, 0:16], J16)
    for j, (nm, tg) in enumerate((("PC", gi_), ("g2", g2), ("g8", g8), ("g21", g21))):
        ts("J " + nm, "EA%d" % j, T.EA[:, 16 * j:16 * j + 16], J16, tg, None, eq)
    ts("J7 PC THF", "RT", T.RT[0:8, :], T.JS[0:8, 16:32], T.PC[0:8, 0:1], T.THF[0:8, 0:1], eq, mul)
    ts("BL", "KL", T.KL[:, 13:256:16], T.LS[:, 0:16], -1.0, float(255 + V), mul, add)
    ts("EA0 EA1 BL", "EB", T.EA[:, 64:96], T.EA[:, 0:32], T.LS[:, 0:1], None, mul)
    ts("EA2 EA3 BL", "EC", T.EA[:, 96:128], T.EA[:, 32:64], T.LS[:, 8:9], None, mul)
    ts("J PC m15", "PK", T.PK[:], T.J[:, 0:8], gi_, m15, eq, mul)
    mm("RT ON", "B3", B[3][:, 0:16], T.ON[0:8, :], T.RT[0:8, :], True, True)
    tt("EB EC", "EB", T.EA[:, 64:96], T.EA[:, 64:96], T.EA[:, 96:128], add)

    OF, K1, NT, XX, DD, VAL, WW, DL, K2 = [T.L[:, 16 * j:16 * j + 16] for j in range(9)]
    P = B[0]
    gb = lambda k: "GB%d" % k
    KV = sum(CHUNKS)
    late = range(KV, 16)

    for r in range(R):
        last = r == R - 1
        off, aln, cc, meta = [T["%s%d" % (x, r)] for x in ("off", "aln", "cc", "meta")]
        koff, kaln, kcn, kmeta = ["%s%d" % (x, r) for x in ("off", "aln", "cn", "meta")]
        kca = "ca%d_1 ca%d_2" % (r, r)
        XK = "X10 X11 X2 " + koff
        act(SK + " " + kaln, "GA0", T.GA[:, 0:2048], T.S[:].indirect(aln[:, 0:128]))
        act(XK, "GX", T.GX[:, 0:256 * (16 - KV)], T.X2[:].indirect(off[:, 16 * KV:256]))
        act(SK + " " + kaln, "GA1", T.GA[:, 2048:4096], T.S[:].indirect(aln[:, 128:256]))
        k0 = 0
        for nk in CHUNKS:
            tt(XK + " " + kca, " ".join(gb(k) for k in range(k0, k0 + nk)), T.GB[:, 256 * k0:256 * (k0 + nk)],
               T.X2[:].indirect(off[:, 16 * k0:16 * (k0 + nk)]), cc[:, 256:256 + 256 * nk], A.min)
            k0 += nk
        if r == 0:
            cp("B3", "TH", T.LS[:, 48:64], B[3][:, 0:16])
        elif not last:
            cp(kaln, "APt", T.AP[:, V:W], aln[:])
        for c in range(2):
            mm(kca + " WC%d" % c, "B0", P[:, 0:256], cc[:, 256 + 128 * c:384 + 128 * c], T.WC[:, 256 * c:256 * c + 256], c == 0, False)

        def mb(ks, src, key, w, k1=0):
            for k in ks:
                for c in range(2):
                    lo = 256 * (k - k1) + 128 * c
                    mm(key(k) + " WB0 WB1", "B0", P[:, 16 * c + k:256:32], src[:, lo:lo + 128], T.WB[:, 8 * w:8 * w + 8], False, False)

        def ma(h, ks, stop=False):
            for k in ks:
                mm("GA%d WA" % h, "B0", P[:, 128 * h + k:128 * h + 128:16], T.GA[:, 2048 * h + k:2048 * h + 2048:16],
                   T.WA[:, k:128:16], False, stop and k == ks[-1])

        ka = 2 if r == 0 else 6
        mb(range(0, ka), T.GB, gb, 0)
        ma(0, range(0, ka))
        for k in range(KV, 16, 2):
            bk = 1 + (k - KV) // 2
            mm("GX IB", "B%d" % bk, B[bk][:], T.IB[:], T.GX[:, 256 * (k - KV):256 * (k - KV + 2)], True, False)
            mm(kca + " NI", "B%d" % bk, B[bk][:], T.NI[:], cc[:, 256:768], False, True)
            act("B%d" % bk, gb(k) + " " + gb(k + 1), T.GB[:, 256 * k:256 * (k + 2)], B[bk][:], F.Relu)
        mb(late, T.GX, lambda k: "GX", 0, KV)
        for k in range(ka, KV - 2, 2):
            mb((k, k + 1), T.GB, gb, 0)
            ma(0, (k, k + 1))
        ma(1, range(0, KV - 2))
        for k in range(KV - 2, 16):
            mb((k,), T.GB, gb, int(k >= KV))
            ma(0, (k,))
            ma(1, (k,), k == 15)
        op("v", "B0 D0", "SC", g.vector.tensor_tensor_scan, T.SC[:], T.D0[:], P[:, 0:256], 0.0, mul, A.max)
        cp("SC", "KI", T.KI[:], T.SC[:, 15:256:16])
        ts("KI", "GI", T.GI[:], T.KI[:], 16, None, A.arith_shift_right)
        ts("KI", "FI", T.FI[:], T.KI[:], 4095, None, A.bitwise_and)
        cp("GI", "KL", T.KL[:, 12:256:16], T.GI[:])
        tt("FI REPO MK", "RK", T.RK[:], T.FI[:].indirect(T.OFS[:, 0:16]), T.MK[:], mul)
        for h in range(2):
            mm("KL IB", "B2", B[2][:, 128 * h:128 * h + 128], T.KL[:, 128 * h:128 * h + 128], T.IB[:], True, True)
        for h in range(2):
            mm("RK EA0 EA2", "B1", B[1][:, 0:16], T.RK[:, 128 * h:128 * h + 128], T.EA[:, 32 * h:32 * h + 16], h == 0, h == 1)
        act("B2 kb", "KS", T.KS[:], B[2][:, 0:256], bias=kb)
        ts("GI", "K1", K1, T.GI[:], -256.0, None, mul)
        tt("GI TH", "OF", OF, T.GI[:], T.LS[:, 48:64], A.is_gt)
        tt("FI BL", "DD", DD, T.FI[:], T.LS[:, 0:16], sub)
        tt("K1 NK", "K2", K2, K1, T.LS[:, 16:32], add)
        ts("GI", "KM", T.KM[:, 14:256:16], T.GI[:], -1.0, None, mul)
        cp("B1", "FO", T.FO[:], B[1][:, 0:16])
        act(SK + " FO", "LE", T.LE[:], T.S[:].indirect(T.FO[:]))
        tt(SK + " FO KS", "RR", T.RR[:], T.S[:].indirect(T.FO[:]), T.KS[:], add)
        tt("K2 OF", "NT", NT, K2, OF, mul)
        ts("LE odd", "LO", T.LO[:], T.LE[:], odd, None, mul)
        tt("NT NV", "XX", XX, NT, T.LS[:, 32:48], mul)
        towns = (0, 2, 4, 6, 1, 3, 5, 7)
        for j, tw in enumerate(towns):
            bk, q = (3 + j) % 8, 32 * (tw // 2)
            src, key, kk = (T.LO, "LO", 32) if tw % 2 else (T.LE, "LE", 14)
            for h in range(2):
                mm(key + " RR", "B%d" % bk, B[bk][:, 256 * h:256 * h + 256], src[q:q + kk, 128 * h:128 * h + 128],
                   T.RR[q:q + kk, :], True, True)
        for j, tw in enumerate(towns):
            bk = (3 + j) % 8
            for h in range(2):
                c = 8 * h + tw
                z = B[bk][:, 256 * h:256 * h + 256]
                if j % 2:
                    op("v", "B%d" % bk, "VAL%d" % c, g.vector.tensor_reduce, T.L[:, 80 + c:81 + c], z, AxisListType.X, A.max)
                else:
                    act("B%d NT" % bk, "VAL%d JK%d" % (c, c), T.MN[:, 256 * (j + h):256 * (j + h + 1)], z,
                        F.Relu, bias=T.L[:, 32 + c:33 + c], accum_out=T.L[:, 80 + c:81 + c])
        mm("MK EB", "B3", B[3][:, 0:32], T.MK[:, 0:128], T.EA[:, 64:96], True, False)
        act(SK + " FO", "G32", T.G32[:], T.S[:].indirect(T.FO[:]))
        tt(" ".join("VAL%d" % c for c in range(16)) + " XX", "WW", WW, VAL, XX, A.is_le)
        for h in range(2):
            mm("G32 PK", "B5", B[5][:, 8 * h:8 * h + 8], T.G32[:, 128 * h:128 * h + 128], T.PK[:], True, True)
        tt("WW DD", "O1", T.O1[:], WW, DD, mul)
        tt("WW " + kmeta, "smeta", T.smeta[:, 16:32], meta[:, 16:32], WW, add)
        tt("O1 REPO MK", "RK", T.RK[:], T.O1[:].indirect(T.OFS[:, 0:16]), T.MK[:], mul)
        for h in range(2):
            mm("RK EA0 EA1 EA2 EA3", "B3", B[3][:, 0:32], T.RK[:, 128 * h:128 * h + 128], T.EA[:, 32 * h:32 * h + 32], False, h == 1)
        tt("B5 " + kmeta, "KM", T.KM[:, 15:256:16], meta[:, 0:16], B[5][:, 0:16], sub)
        tt("KM WW", "DL", DL, T.KM[:, 15:256:16], WW, mul)
        tt("DL " + kmeta, "smeta", T.smeta[:, 0:16], meta[:, 0:16], DL, sub)
        meta_out = lambda: send("m%d" % r, "smeta", "meta%d" % (r + 1), T.smeta[:], T["meta%d" % (r + 1)][:])
        if r == 0 or last:
            meta_out()

        for h in range(2):
            mm("KM IF", "B6", B[6][:, 128 * h:128 * h + 128], T.KM[:, 128 * h:128 * h + 128], T.IF[:], True, True)
        cp("B3", "O", T.O[:], B[3][:, 0:32])
        if not last:
            nx = lambda x: T["%s%d" % (x, r + 1)]
            act("Y0 Y1 Yt O", "scn", T.scc[:, 0:256], T.Y[:].indirect(T.O[:, 0:16]))
            features_out(T.scc, "scn", "sca")
            cp("AP APt O", "saln", T.saln[:], T.AP[:].indirect(T.O[:, 0:16]))
            send("a%d" % r, "saln", "aln%d" % (r + 1), T.saln[:], nx("aln")[:])
            turn(T.AP[:], "AP APt", T.soff[:], "soff")
            send("c%d" % r, "scn sca_1 sca_2", "cn%d ca%d_1 ca%d_2" % (r + 1, r + 1, r + 1), T.scc[:], nx("cc")[:])
            send("b%d" % r, "soff", "off%d" % (r + 1), T.soff[:], nx("off")[:])
            if r > 0:
                meta_out()
        tt("G32 B6", "NN", T.NN[:], T.G32[:], B[6][:, 0:256], add)
        cp("NN O", SK, T.S[:].indirect(T.O[:, 0:16]), T.NN[:])
        if r < R - 2:
            cp(kaln + " O", "AP APt", T.AP[:].indirect(T.O[:, 0:16]), aln[:])
            cp(kcn + " O", "Y0 Y1 Yt", T.Y[:].indirect(T.O[:, 0:16]), cc[:, 0:256])
            dma("y", "yc%d" % r, "cn%d" % (r + 1), "Yt", [(T.Y[:, V:W], nx("cc")[:, 0:256])])

    dma("y", "o1", SK, "", [(T.yh[:], T.S[15:128:16, 0:V])])
    mm("meta%d IF" % R, "B7", B[7][0:32, 0:128], T["meta%d" % R][:], T.IF[:], True, True)
    act("B7", "OUT", T.OUT[0:32, :], B[7][0:32, 0:128])
    dma("s", "o2", "OUT", "", [(y[:, 128 * h:128 * h + 128], T.OUT[16 * j + 8 * h:16 * j + 8 * h + 8, :])
                               for j, y in enumerate((T.yt, T.yl)) for h in range(2)])
    for sem, val in count.items():
        need("g", (sem, val))
